import numpy as np
import ml_dtypes


def mxq(x, axis, fmt="e4m3"):
    dtype, down = {"e4m3": (ml_dtypes.float8_e4m3fn, 7), "e5m2": (ml_dtypes.float8_e5m2, 14)}[fmt]
    v = np.moveaxis(np.asarray(x, np.float32).astype(ml_dtypes.bfloat16).astype(np.float64), axis, -1)
    blocks = v.reshape(v.shape[:-1] + (-1, 32))
    amax = np.abs(blocks).max(-1, keepdims=True)
    byte = np.maximum(np.where(amax > 0, np.frexp(amax)[1] - 1 + 127, 0) - down, 1)
    scale = np.exp2(byte - 127.0)
    codes = (blocks / scale).astype(np.float32).astype(dtype).astype(np.float64)
    return np.moveaxis((codes * scale).reshape(v.shape), -1, axis)


WIDE = False


def mx_kscale(k, group=512):
    if not WIDE:
        return np.ones(k)
    levels = np.array([18, -18])
    if group != 512:
        return np.exp2(np.random.permutation(np.resize(levels, k // group))).repeat(group)
    if k % 512:
        return np.exp2(np.random.permutation(np.resize(levels, k // 32))).repeat(32)
    a = np.empty((k // 512, 16))
    for p in range(k // 512):
        a[p, :8] = np.random.permutation(np.resize(levels, 8))
        for g in range(8):
            far = levels[np.abs(levels - a[p, g]) >= 10]
            a[p, g + 8] = far[np.random.randint(len(far))]
    return np.exp2(a.ravel()).repeat(32)


def f64(x):
    return np.asarray(x).astype(np.float64)


def sigmoid(v):
    return 1.0 / (1.0 + np.exp(-v))


G, D, M, N = 4, 128, 128, 512


def setup_inputs():
    n = np.random.standard_normal
    s_d = mx_kscale(D, 0)
    return {
        "x": (n((G, D, N)) * s_d[:, None]).astype(np.float32),
        "w1": (n((G, D, M)) / np.sqrt(D) / s_d[:, None]).astype(np.float32),
        "w2": (n((G, D, M)) / np.sqrt(D) / s_d[:, None]).astype(np.float32),
        "gn": (np.random.uniform(0.5, 2.0, (G, M, 1))).astype(np.float32),
        "dx": (n((G, D, N)) * s_d[:, None]).astype(np.float32),
        "og": (np.random.uniform(0.5, 2.0, (G, M, 1))).astype(np.float32),
        "base": (0.3 * n((G, M, N))).astype(np.float32),
    }


def reference(x, w1, w2, gn, dx, og, base):
    w1q = mxq(f64(w1), 1, "e4m3")
    xq = mxq(f64(x), 1, "e4m3")
    z1 = w1q.transpose(0, 2, 1) @ xq
    dxq = mxq(f64(dx), 1, "e4m3")
    tz1 = w1q.transpose(0, 2, 1) @ dxq
    w2q = mxq(f64(w2), 1, "e4m3")
    z2 = w2q.transpose(0, 2, 1) @ xq
    tz2 = w2q.transpose(0, 2, 1) @ dxq
    rm = np.sqrt(np.mean(np.square(z1), axis=-1, keepdims=True) + 0.01)
    nz = z1 / rm * f64(gn)
    xrm = np.mean(tz1 * z1 * 2.0, axis=-1, keepdims=True) * 0.5 / rm
    xnz = (tz1 - xrm * z1 / rm) / rm * f64(gn)
    xh = xnz * sigmoid(z2) + tz2 * sigmoid(z2) * (1.0 - sigmoid(z2)) * nz
    y = xh * f64(og) + f64(base)
    return y

from contextlib import ExitStack

import concourse.mybir as mybir

G, D, M, N = 4, 128, 128, 512
FLOPS = 4 * 2 * G * D * M * N

F32 = mybir.dt.float32
BF16 = mybir.dt.bfloat16
U32 = mybir.dt.uint32
U8 = mybir.dt.uint8
FP8X4 = mybir.dt.float8_e4m3fn_x4
ALU = mybir.AluOpType
ACT = mybir.ActivationFunctionType

P = 128
PACK = 4
ROWS = D // PACK
EPS = 0.01
X_SPLIT = 320
HALF = N // 2


def tile_rows_tnrownorm_kernel(tc, x, w1, w2, gn, dx, og, base, out):
    nc = tc.nc

    def rows_of(t):
        return t.rearrange("g (p j) c -> (g p) j c", j=PACK)

    def interleave(copy, dst, src):
        copy(
            out=dst.rearrange("p (c i) j -> p c j i", i=4),
            in_=src.rearrange("p j (c i) -> p c j i", i=4),
        )

    def quantize(codes, scales, grouped):
        nc.vector.quantize_mx(
            out=codes.bitcast(FP8X4), scales=scales, in_=grouped.rearrange("p c j -> p (c j)")
        )

    with ExitStack() as ctx:
        sb = ctx.enter_context(tc.tile_pool(name="sb", bufs=1))
        ps = ctx.enter_context(tc.psum_pool(name="ps", bufs=1))
        ctx.enter_context(tc.manual_schedule())

        def tiles(name, shape=(P, N), dtype=F32, count=G):
            return [sb.tile(list(shape), dtype, name="%s%d" % (name, i), align_bytes=64) for i in range(count)]

        x_raw = sb.tile([P, PACK, N], F32, name="x_raw", align_bytes=64)
        dx_raw = tiles("dx_raw", (P, PACK, HALF), F32, 2)
        w_raw = tiles("w_raw", (P, PACK, M), F32, 2)
        base_sb = sb.tile([P, G, N], F32, name="base_sb", align_bytes=64)
        x_bf = sb.tile([P, N, PACK], BF16, name="x_bf", align_bytes=64)
        dx_bf = tiles("dx_bf", (P, HALF, PACK), BF16, 2)
        w_bf = tiles("w_bf", (P, M, PACK), BF16, 2)
        x_codes = sb.tile([P, N], U32, name="x_codes", align_bytes=64)
        x_scales = sb.tile([P, N], U8, name="x_scales", align_bytes=64)
        dx_codes = sb.tile([P, N], U32, name="dx_codes", align_bytes=64)
        dx_scales = sb.tile([P, N], U8, name="dx_scales", align_bytes=64)
        w_codes = tiles("w_codes", (P, M), U32, 2)
        w_scales = tiles("w_scales", (P, M), U8, 2)
        gain_rows = sb.tile([P, P], F32, name="gain_rows", align_bytes=64)
        gain_cols = sb.tile([P, P], F32, name="gain_cols", align_bytes=64)
        half_gain = sb.tile([P, G], F32, name="half_gain", align_bytes=64)
        minus_half = sb.tile([P, G], F32, name="minus_half", align_bytes=64)
        sumsq = sb.tile([P, G], F32, name="sumsq", align_bytes=64)
        meansq = sb.tile([P, G], F32, name="meansq", align_bytes=64)
        rstd = sb.tile([P, G], F32, name="rstd", align_bytes=64)
        rvar = sb.tile([P, G], F32, name="rvar", align_bytes=64)
        kh = sb.tile([P, G], F32, name="kh", align_bytes=64)
        c2 = sb.tile([P, G], F32, name="c2", align_bytes=64)
        th = tiles("th")
        sq = tiles("sq")
        z1s = tiles("z1s")
        prod = tiles("prod")
        gate = tiles("gate", count=2)
        a = tiles("a")
        b = tiles("b")
        d = tiles("d")
        e = tiles("e")
        res = tiles("res")
        bank_z1 = [ps.tile([M, N], F32, name="bank_z1_%d" % g) for g in range(G)]
        bank_b = [ps.tile([M, N], F32, name="bank_b_%d" % g) for g in range(G)]

        def product(bank, wi, codes, scales, g):
            r = slice(ROWS * g, ROWS * (g + 1))
            nc.tensor.matmul_mx(
                out=bank[g][:],
                lhsT=w_codes[wi][r, :].bitcast(FP8X4),
                lhsT_scale=w_scales[wi][r, :],
                rhs=codes[r, :].bitcast(FP8X4),
                rhs_scale=scales[r, :],
                start=True,
                stop=True,
            )

        nc.gpsimd.memset(gain_rows[:], 0.0)
        nc.gpsimd.memset(minus_half[:], -0.5)
        nc.sync.dma_start(out=x_raw[:], in_=rows_of(x))
        nc.sync.dma_start(out=w_raw[1][:], in_=rows_of(w2))
        nc.sync.dma_start(out=w_raw[0][:], in_=rows_of(w1))
        for h in range(2):
            nc.sync.dma_start(out=dx_raw[h][:], in_=rows_of(dx)[:, :, HALF * h : HALF * (h + 1)])
        nc.sync.dma_start(out=base_sb[:], in_=base.rearrange("g m n -> m g n"))
        for row, vec in enumerate((gn, og)):
            nc.scalar.dma_start(
                out=gain_rows[row:P:32, :].rearrange("q (g i) -> q g i", i=32),
                in_=vec.rearrange("g (q i) o -> q g (i o)", i=32),
            )
        interleave(nc.vector.tensor_copy, x_bf[:, 0:X_SPLIT, :], x_raw[:, :, 0:X_SPLIT])
        interleave(nc.scalar.copy, x_bf[:, X_SPLIT:N, :], x_raw[:, :, X_SPLIT:N])
        quantize(x_codes[:], x_scales[:], x_bf[:])
        for wi in (1, 0):
            interleave(nc.scalar.copy, w_bf[wi][:], w_raw[wi][:])
            quantize(w_codes[wi][:], w_scales[wi][:], w_bf[wi][:])

        for g in range(G):
            product(bank_b, 1, x_codes, x_scales, g)
            product(bank_z1, 0, x_codes, x_scales, g)

        nc.vector.transpose(out=gain_cols[:], in_=gain_rows[:])
        cols = gain_cols[:].rearrange("p (g i) -> p g i", i=32)
        nc.vector.scalar_tensor_tensor(
            out=half_gain[:].unsqueeze(2), in0=cols[:, :, 0:1], scalar=0.5, in1=cols[:, :, 1:2],
            op0=ALU.mult, op1=ALU.mult,
        )

        for h in range(2):
            interleave(nc.vector.tensor_copy, dx_bf[h][:], dx_raw[h][:])
            cs = slice(HALF * h, HALF * (h + 1))
            quantize(dx_codes[:, cs], dx_scales[:, cs], dx_bf[h][:])

        def tanh_half(g):
            nc.scalar.activation(out=th[g][:], in_=bank_b[g][:], func=ACT.Tanh, scale=0.5)

        def square_sum(g):
            nc.scalar.activation(out=sq[g][:], in_=bank_z1[g][:], func=ACT.Square, accum_out=sumsq[:, g : g + 1])

        def copy_z1(g):
            nc.scalar.activation(out=z1s[g][:], in_=bank_z1[g][:], func=ACT.Copy, scale=2.0 / N)

        def row_stats(gs):
            nc.gpsimd.tensor_scalar(out=meansq[:, gs], in0=sumsq[:, gs], scalar1=1.0 / N, scalar2=EPS, op0=ALU.mult, op1=ALU.add)
            nc.gpsimd.tensor_tensor(out=rstd[:, gs], in0=meansq[:, gs], in1=minus_half[:, gs], op=ALU.pow)
            nc.gpsimd.tensor_tensor(out=rvar[:, gs], in0=rstd[:, gs], in1=rstd[:, gs], op=ALU.mult)
            nc.gpsimd.tensor_tensor(out=kh[:, gs], in0=rstd[:, gs], in1=half_gain[:, gs], op=ALU.mult)

        def make_gate(g):
            col = kh[:, g : g + 1]
            nc.scalar.activation(out=gate[g][:], in_=th[g][:], func=ACT.Identity, scale=col, bias=col)

        def step_a(g):
            nc.vector.scalar_tensor_tensor(out=a[g][:], in0=th[g][:], scalar=1.0, in1=bank_b[g][:], op0=ALU.subtract, op1=ALU.mult)

        def step_c(g):
            nc.vector.scalar_tensor_tensor(
                out=prod[g][:], in0=bank_b[g][:], scalar=rvar[:, g : g + 1], in1=z1s[g][:],
                op0=ALU.mult, op1=ALU.mult, accum_out=c2[:, g : g + 1],
            )

        def step_b(g):
            nc.vector.scalar_tensor_tensor(out=b[g][:], in0=a[g][:], scalar=c2[:, g : g + 1], in1=bank_z1[g][:], op0=ALU.add, op1=ALU.mult)

        def step_d(g):
            nc.vector.scalar_tensor_tensor(out=d[g][:], in0=b[g][:], scalar=-0.5, in1=bank_b[g][:], op0=ALU.mult, op1=ALU.add)

        def store(g):
            nc.sync.dma_start(out=out[g], in_=res[g][:])

        def front(pair):
            for g in pair:
                tanh_half(g)
                square_sum(g)
            row_stats(slice(pair[0], pair[-1] + 1))
            for g in pair:
                copy_z1(g)

        def middle(pair):
            for g in pair:
                product(bank_b, 1, dx_codes, dx_scales, g)
            for g in pair:
                step_a(g)
                product(bank_b, 0, dx_codes, dx_scales, g)
            for step in (step_c, step_b, step_d):
                for g in pair:
                    step(g)

        first, second = (0, 1), (2, 3)
        front(first)
        front(second)
        middle(first)
        for g in first:
            make_gate(g)
            nc.gpsimd.tensor_tensor(out=e[g][:], in0=d[g][:], in1=gate[g][:], op=ALU.mult)
            nc.gpsimd.tensor_tensor(out=res[g][:], in0=e[g][:], in1=base_sb[:, g, :], op=ALU.add)
            store(g)
        middle(second)
        for g in second:
            nc.vector.scalar_tensor_tensor(out=e[g][:], in0=th[g][:], scalar=1.0, in1=d[g][:], op0=ALU.add, op1=ALU.mult)
        for g in second:
            nc.vector.scalar_tensor_tensor(out=res[g][:], in0=e[g][:], scalar=kh[:, g : g + 1], in1=base_sb[:, g, :], op0=ALU.mult, op1=ALU.add)
            store(g)
